import numpy as np
import ml_dtypes


def mxq(x, axis, fmt="e4m3"):
    dtype, down = {"e4m3": (ml_dtypes.float8_e4m3fn, 7), "e5m2": (ml_dtypes.float8_e5m2, 14)}[fmt]
    v = np.moveaxis(np.asarray(x, np.float32).astype(ml_dtypes.bfloat16).astype(np.float64), axis, -1)
    blocks = v.reshape(v.shape[:-1] + (-1, 32))
    amax = np.abs(blocks).max(-1, keepdims=True)
    byte = np.maximum(np.where(amax > 0, np.frexp(amax)[1] - 1 + 127, 0) - down, 1)
    scale = np.exp2(byte - 127.0)
    codes = (blocks / scale).astype(np.float32).astype(dtype).astype(np.float64)
    return np.moveaxis((codes * scale).reshape(v.shape), -1, axis)


WIDE = False


def mx_kscale(k):
    if not WIDE:
        return np.ones(k)
    levels = np.array([10, -10, 5, -5, 0])
    if k % 512:
        return np.exp2(np.random.permutation(np.resize(levels, k // 32))).repeat(32)
    a = np.empty((k // 512, 16))
    for p in range(k // 512):
        a[p, :8] = np.random.permutation(np.resize(levels, 8))
        for g in range(8):
            far = levels[np.abs(levels - a[p, g]) >= 10]
            a[p, g + 8] = far[np.random.randint(len(far))]
    return np.exp2(a.ravel()).repeat(32)


def f64(x):
    return np.asarray(x).astype(np.float64)


def striped(idx):
    return np.tile(idx.reshape(-1, 16).T, (8, 1)).astype(np.uint16)


def unstriped(offs):
    return offs[:16].T.reshape(-1).astype(np.int64)


def pack_weight(w):
    k, n = w.shape
    w = f64(np.asarray(w, np.float32).astype(ml_dtypes.bfloat16)).reshape(k // 32, 32, n)
    amax = np.abs(w).max(1)
    byte = np.clip(np.where(amax > 0, np.frexp(amax)[1] - 1 + 127 - 7, 1), 1, 254)
    scaled = (w * np.exp2(127.0 - byte)[:, None, :]).reshape(k, n).astype(np.float32)
    words = np.ascontiguousarray(scaled.reshape(k // 512, 128, 4, n).transpose(0, 1, 3, 2)).astype(ml_dtypes.float8_e4m3fn).view(np.uint8)
    return words, np.ascontiguousarray(byte.astype(np.uint8).reshape(k // 512, 16, n))


def unpack_weight(words, scales):
    g, p, n, _ = words.shape
    vals = np.ascontiguousarray(words).view(ml_dtypes.float8_e4m3fn).astype(np.float64) * np.repeat(np.exp2(scales.astype(np.float64) - 127.0), 8, axis=1)[..., None]
    return vals.transpose(0, 1, 3, 2).reshape(g * 512, n)


def silu(v):
    return v / (1.0 + np.exp(-np.maximum(v, -700.0)))


K, T, E, C, N = 2048, 512, 4, 128, 128


def by_expert(wq, xq):
    return np.concatenate([wq[e].T @ xq[:, e * C:(e + 1) * C] for e in range(E)], axis=1)


def setup_inputs():
    n = np.random.standard_normal
    s = mx_kscale(K)[:, None]
    packed = [pack_weight(m) for m in n((E, K, N)) / np.sqrt(K) / s[None]]
    return {
        "xT": (n((K, T)) * s).astype(np.float32),
        "w_words": np.stack([m[0] for m in packed]),
        "w_scales": np.stack([m[1] for m in packed]),
        "b": (0.3 * n((N, E))).astype(np.float32),
        "gate": np.tile(np.random.uniform(0.2, 1.0, E * C), (N, 1)).astype(np.float32),
        "offs": striped(np.random.permutation(T)[:E * C]),
    }


def reference(xT, w_words, w_scales, b, gate, offs):
    idx = unstriped(offs)
    xq = mxq(f64(xT)[:, idx], 0, "e4m3")
    w = np.stack([unpack_weight(w_words[e], w_scales[e]) for e in range(E)])
    y = by_expert(w, xq)
    y = silu(y + np.repeat(f64(b), C, axis=1))
    out = np.zeros((N, T))
    out[:, idx] = f64(gate) * y
    return out

@@ -1,0 +1,129 @@
+from contextlib import ExitStack
+
+import concourse.mybir as mybir
+
+K, T, E, C, N = 2048, 512, 4, 128, 128
+FLOPS = 2 * K * N * E * C
+
+F32 = mybir.dt.float32
+BF16 = mybir.dt.bfloat16
+I32 = mybir.dt.int32
+U32 = mybir.dt.uint32
+U16 = mybir.dt.uint16
+U8 = mybir.dt.uint8
+FP8X4 = mybir.dt.float8_e4m3fn_x4
+
+P = 128
+PACK = 4
+PASSES = K // (P * PACK)
+HALF = 256
+HALVES = E * C // HALF
+EXPERTS_PER_HALF = HALF // C
+OFFS_COLS = HALF // 16
+
+
+def tile_routed_moe_kernel(tc, xT, w_words, w_scales, b, gate, offs, out):
+    nc = tc.nc
+    silu = mybir.ActivationFunctionType.Silu
+    mult = mybir.AluOpType.mult
+
+    with ExitStack() as ctx:
+        held = ctx.enter_context(tc.tile_pool(name="held", bufs=1))
+        psum = ctx.enter_context(tc.psum_pool(name="psum", bufs=1))
+
+        offsets = held.tile([P, E * C // 16], U16, name="offsets")
+        nc.sync.dma_start(offsets[:], offs)
+
+        zero = held.tile([P, 1], F32, name="zero")
+        warm = held.tile([P, 1], F32, name="warm")
+        nc.gpsimd.memset(zero[:], 0.0)
+        nc.scalar.activation(out=warm[:], in_=zero[:], func=silu)
+
+        w_planes = held.tile([P, E * PASSES, N], U8, name="w_planes", align_bytes=64)
+        nc.vector.memset(w_planes[:].rearrange("p a n -> p (a n)").bitcast(I32), 0)
+
+        x_view = xT.rearrange("(g p t) n -> g p t n", p=P, t=PACK)
+        planes = {}
+
+        def load_pass(g):
+            for t in range(PACK):
+                plane = held.tile([P, T], F32, name="plane%d_%d" % (g, t))
+                nc.sync.dma_start(plane[:], x_view[g, :, t, :])
+                planes[(g, t)] = plane
+
+        load_pass(0)
+        load_pass(1)
+
+        s_view = w_scales.bitcast(I32).rearrange("e a (q r) n -> r q (e a) n", r=4)
+        for r in range(4):
+            nc.sync.dma_start(w_planes[r:P:32, :, :].bitcast(I32), s_view[r])
+
+        w_view = w_words.rearrange("e a p n r -> a p e (n r)").bitcast(I32)
+        w_codes = []
+        for a in range(PASSES):
+            codes = held.tile([P, E, N], U32, name="w_codes%d" % a, align_bytes=64)
+            nc.sync.dma_start(codes[:].bitcast(I32), w_view[a])
+            w_codes.append(codes)
+
+        b_sb = held.tile([P, E], F32, name="b_sb")
+        nc.sync.dma_start(b_sb[:], b)
+        load_pass(2)
+        load_pass(3)
+        gate_sb = held.tile([P, E * C], F32, name="gate_sb")
+        nc.sync.dma_start(gate_sb[:], gate)
+
+        acc = [psum.tile([P, C], F32, name="acc%d" % e) for e in range(E)]
+        window = held.tile([P, T], F32, name="window")
+
+        units = [(g, h) for g in range(PASSES) for h in range(HALVES)]
+        grouped = {}
+
+        def offs_of(h):
+            return offsets[:, h * OFFS_COLS : (h + 1) * OFFS_COLS]
+
+        def gather(g, h):
+            g4 = held.tile([P, PACK, HALF], F32, name="g4_%d_%d" % (g, h))
+            for t in range(PACK):
+                nc.vector.tensor_copy(out=g4[:, t, :], in_=planes[(g, t)][:].indirect(offs_of(h)))
+            grp = held.tile([P, HALF, PACK], BF16, name="grp_%d_%d" % (g, h), align_bytes=64)
+            nc.scalar.copy(out=grp[:], in_=g4[:].rearrange("p t n -> p n t"))
+            grouped[(g, h)] = grp
+
+        def multiply(g, h):
+            x_codes = held.tile([P, HALF], U32, name="x_codes_%d_%d" % (g, h), align_bytes=64)
+            x_planes = held.tile([P, HALF], U8, name="x_planes_%d_%d" % (g, h), align_bytes=64)
+            nc.vector.quantize_mx(
+                out=x_codes[:].bitcast(FP8X4),
+                scales=x_planes[:],
+                in_=grouped[(g, h)][:].rearrange("p n t -> p (n t)"),
+            )
+            for i in range(EXPERTS_PER_HALF):
+                e = h * EXPERTS_PER_HALF + i
+                nc.tensor.matmul_mx(
+                    out=acc[e][:],
+                    lhsT=w_codes[g][:, e, :].bitcast(FP8X4),
+                    lhsT_scale=w_planes[:, e * PASSES + g, :],
+                    rhs=x_codes[:, i * C : (i + 1) * C].bitcast(FP8X4),
+                    rhs_scale=x_planes[:, i * C : (i + 1) * C],
+                    start=(g == 0),
+                    stop=(g == PASSES - 1),
+                )
+
+        def finish(h):
+            y = held.tile([P, HALF], F32, name="y%d" % h)
+            for i in range(EXPERTS_PER_HALF):
+                e = h * EXPERTS_PER_HALF + i
+                nc.scalar.activation(out=y[:, i * C : (i + 1) * C], in_=acc[e][:], func=silu, bias=b_sb[:, e : e + 1])
+            nc.vector.tensor_tensor(
+                out=window[:].indirect(offs_of(h)), in0=y[:], in1=gate_sb[:, h * HALF : (h + 1) * HALF], op=mult
+            )
+
+        gather(*units[0])
+        for i in range(1, len(units)):
+            gather(*units[i])
+            multiply(*units[i - 1])
+        multiply(*units[-1])
+        for h in range(HALVES):
+            finish(h)
+
+        nc.sync.dma_start(out, window[:])

@@ -16,16 +16,16 @@ FP8X4 = mybir.dt.float8_e4m3fn_x4
 P = 128
 PACK = 4
 PASSES = K // (P * PACK)
+
 HALF = 256
-HALVES = E * C // HALF
-EXPERTS_PER_HALF = HALF // C
-OFFS_COLS = HALF // 16
 
 
 def tile_routed_moe_kernel(tc, xT, w_words, w_scales, b, gate, offs, out):
     nc = tc.nc
     silu = mybir.ActivationFunctionType.Silu
+    copy = mybir.ActivationFunctionType.Copy
     mult = mybir.AluOpType.mult
+    add = mybir.AluOpType.add
 
     with ExitStack() as ctx:
         held = ctx.enter_context(tc.tile_pool(name="held", bufs=1))
@@ -43,87 +43,111 @@ def tile_routed_moe_kernel(tc, xT, w_words, w_scales, b, gate, offs, out):
         nc.vector.memset(w_planes[:].rearrange("p a n -> p (a n)").bitcast(I32), 0)
 
         x_view = xT.rearrange("(g p t) n -> g p t n", p=P, t=PACK)
-        planes = {}
+        raw = [held.tile([P, PACK, T], F32, name="raw%d" % g) for g in range(PASSES)]
+        xb = {g: held.tile([P, PACK, T], BF16, name="xb%d" % g) for g in (2, 3)}
 
-        def load_pass(g):
-            for t in range(PACK):
-                plane = held.tile([P, T], F32, name="plane%d_%d" % (g, t))
-                nc.sync.dma_start(plane[:], x_view[g, :, t, :])
-                planes[(g, t)] = plane
-
-        load_pass(0)
-        load_pass(1)
+        for i in range(8):
+            for g in (i // PACK, 2 + i // PACK):
+                nc.sync.dma_start(raw[g][:, i % PACK, :], x_view[g, :, i % PACK, :])
 
         s_view = w_scales.bitcast(I32).rearrange("e a (q r) n -> r q (e a) n", r=4)
         for r in range(4):
             nc.sync.dma_start(w_planes[r:P:32, :, :].bitcast(I32), s_view[r])
-
         w_view = w_words.rearrange("e a p n r -> a p e (n r)").bitcast(I32)
-        w_codes = []
-        for a in range(PASSES):
-            codes = held.tile([P, E, N], U32, name="w_codes%d" % a, align_bytes=64)
-            nc.sync.dma_start(codes[:].bitcast(I32), w_view[a])
-            w_codes.append(codes)
-
+        w_codes = {}
+        for a in (0, 2, 1, 3):
+            w_codes[a] = held.tile([P, E, N], U32, name="w_codes%d" % a, align_bytes=64)
+            nc.sync.dma_start(w_codes[a][:].bitcast(I32), w_view[a])
         b_sb = held.tile([P, E], F32, name="b_sb")
         nc.sync.dma_start(b_sb[:], b)
-        load_pass(2)
-        load_pass(3)
         gate_sb = held.tile([P, E * C], F32, name="gate_sb")
         nc.sync.dma_start(gate_sb[:], gate)
 
         acc = [psum.tile([P, C], F32, name="acc%d" % e) for e in range(E)]
         window = held.tile([P, T], F32, name="window")
-
-        units = [(g, h) for g in range(PASSES) for h in range(HALVES)]
         grouped = {}
+        pass_order = (0, 2, 1, 3)
 
         def offs_of(h):
-            return offsets[:, h * OFFS_COLS : (h + 1) * OFFS_COLS]
+            return offsets[:, h * (HALF // 16) : (h + 1) * (HALF // 16)]
 
-        def gather(g, h):
-            g4 = held.tile([P, PACK, HALF], F32, name="g4_%d_%d" % (g, h))
-            for t in range(PACK):
-                nc.vector.tensor_copy(out=g4[:, t, :], in_=planes[(g, t)][:].indirect(offs_of(h)))
-            grp = held.tile([P, HALF, PACK], BF16, name="grp_%d_%d" % (g, h), align_bytes=64)
-            nc.scalar.copy(out=grp[:], in_=g4[:].rearrange("p t n -> p n t"))
-            grouped[(g, h)] = grp
+        def group_tile(g, h):
+            if (g, h) not in grouped:
+                grouped[(g, h)] = held.tile([P, HALF, PACK], BF16, name="grp%d_%d" % (g, h), align_bytes=64)
+            return grouped[(g, h)]
+
+        def cast(g, t):
+            nc.gpsimd.tensor_scalar(out=xb[g][:, t, :], in0=raw[g][:, t, :], scalar1=1.0, scalar2=0.0, op0=mult, op1=add)
+
+        def gather_v(g, t, h):
+            nc.vector.tensor_copy(out=group_tile(g, h)[:, :, t], in_=raw[g][:, t, :].indirect(offs_of(h)))
+
+        def gather_s(g, t, h):
+            nc.scalar.activation(out=group_tile(g, h)[:, :, t], in_=xb[g][:, t, :].indirect(offs_of(h)), func=copy)
 
         def multiply(g, h):
-            x_codes = held.tile([P, HALF], U32, name="x_codes_%d_%d" % (g, h), align_bytes=64)
-            x_planes = held.tile([P, HALF], U8, name="x_planes_%d_%d" % (g, h), align_bytes=64)
+            x_codes = held.tile([P, HALF], U32, name="x_codes%d_%d" % (g, h), align_bytes=64)
+            x_planes = held.tile([P, HALF], U8, name="x_planes%d_%d" % (g, h), align_bytes=64)
             nc.vector.quantize_mx(
-                out=x_codes[:].bitcast(FP8X4),
-                scales=x_planes[:],
-                in_=grouped[(g, h)][:].rearrange("p n t -> p (n t)"),
+                out=x_codes[:].bitcast(FP8X4), scales=x_planes[:], in_=grouped[(g, h)][:].rearrange("p n t -> p (n t)")
             )
-            for i in range(EXPERTS_PER_HALF):
-                e = h * EXPERTS_PER_HALF + i
+            for i in range(HALF // C):
+                e = h * (HALF // C) + i
                 nc.tensor.matmul_mx(
                     out=acc[e][:],
                     lhsT=w_codes[g][:, e, :].bitcast(FP8X4),
                     lhsT_scale=w_planes[:, e * PASSES + g, :],
                     rhs=x_codes[:, i * C : (i + 1) * C].bitcast(FP8X4),
                     rhs_scale=x_planes[:, i * C : (i + 1) * C],
-                    start=(g == 0),
-                    stop=(g == PASSES - 1),
+                    start=(g == pass_order[0]),
+                    stop=(g == pass_order[-1]),
                 )
 
-        def finish(h):
-            y = held.tile([P, HALF], F32, name="y%d" % h)
-            for i in range(EXPERTS_PER_HALF):
-                e = h * EXPERTS_PER_HALF + i
-                nc.scalar.activation(out=y[:, i * C : (i + 1) * C], in_=acc[e][:], func=silu, bias=b_sb[:, e : e + 1])
+        y = [held.tile([P, HALF], F32, name="y%d" % h) for h in range(2)]
+
+        def activate(h):
+            for i in range(HALF // C):
+                e = h * (HALF // C) + i
+                nc.scalar.activation(out=y[h][:, i * C : (i + 1) * C], in_=acc[e][:], func=silu, bias=b_sb[:, e : e + 1])
+
+        def scatter(h):
             nc.vector.tensor_tensor(
-                out=window[:].indirect(offs_of(h)), in0=y[:], in1=gate_sb[:, h * HALF : (h + 1) * HALF], op=mult
+                out=window[:].indirect(offs_of(h)), in0=y[h][:], in1=gate_sb[:, h * HALF : (h + 1) * HALF], op=mult
             )
 
-        gather(*units[0])
-        for i in range(1, len(units)):
-            gather(*units[i])
-            multiply(*units[i - 1])
-        multiply(*units[-1])
-        for h in range(HALVES):
-            finish(h)
+        for g in (2, 3):
+            for t in range(PACK):
+                cast(g, t)
+        for t in range(PACK):
+            for h in range(2):
+                gather_v(0, t, h)
+        for t in range(PACK):
+            for h in range(2):
+                gather_s(2, t, h)
+        gather_v(1, 0, 0)
+        multiply(0, 0)
+        gather_v(1, 0, 1)
+        multiply(0, 1)
+        for t in (1, 2):
+            for h in range(2):
+                gather_v(1, t, h)
+        multiply(2, 0)
+        gather_v(1, 3, 0)
+        multiply(2, 1)
+        gather_v(1, 3, 1)
+        for t in range(PACK):
+            gather_s(3, t, 0)
+        multiply(1, 0)
+        multiply(1, 1)
+        multiply(3, 0)
+        gather_s(3, 0, 1)
+        gather_s(3, 1, 1)
+        activate(0)
+        gather_s(3, 2, 1)
+        gather_s(3, 3, 1)
+        scatter(0)
+        multiply(3, 1)
+        activate(1)
+        scatter(1)
 
         nc.sync.dma_start(out, window[:])

@@ -71,21 +71,31 @@ def tile_routed_moe_kernel(tc, xT, w_words, w_scales, b, gate, offs, out):
         def offs_of(h):
             return offsets[:, h * (HALF // 16) : (h + 1) * (HALF // 16)]
 
-        def group_tile(g, h):
-            if (g, h) not in grouped:
-                grouped[(g, h)] = held.tile([P, HALF, PACK], BF16, name="grp%d_%d" % (g, h), align_bytes=64)
-            return grouped[(g, h)]
+        paired = {}
+
+        def pair_tile(g, h):
+            if (g, h) not in paired:
+                paired[(g, h)] = held.tile([P, 2, HALF, 2], BF16, name="pair%d_%d" % (g, h), align_bytes=64)
+            return paired[(g, h)]
+
+        def merge(g, h, engine_copy):
+            grouped[(g, h)] = held.tile([P, HALF, PACK], BF16, name="grp%d_%d" % (g, h), align_bytes=64)
+            engine_copy(
+                out=grouped[(g, h)][:].rearrange("p s t -> p (s t)").bitcast(F32).rearrange("p (s u) -> p s u", u=2),
+                in_=paired[(g, h)][:].rearrange("p u s e -> p (u s e)").bitcast(F32).rearrange("p (u s) -> p s u", u=2),
+            )
 
         def cast(g, t):
             nc.gpsimd.tensor_scalar(out=xb[g][:, t, :], in0=raw[g][:, t, :], scalar1=1.0, scalar2=0.0, op0=mult, op1=add)
 
         def gather_v(g, t, h):
-            nc.vector.tensor_copy(out=group_tile(g, h)[:, :, t], in_=raw[g][:, t, :].indirect(offs_of(h)))
+            nc.vector.tensor_copy(out=pair_tile(g, h)[:, t // 2, :, t % 2], in_=raw[g][:, t, :].indirect(offs_of(h)))
 
         def gather_s(g, t, h):
-            nc.scalar.activation(out=group_tile(g, h)[:, :, t], in_=xb[g][:, t, :].indirect(offs_of(h)), func=copy)
+            nc.scalar.activation(out=pair_tile(g, h)[:, t // 2, :, t % 2], in_=xb[g][:, t, :].indirect(offs_of(h)), func=copy)
 
         def multiply(g, h):
+            merge(g, h, nc.vector.tensor_copy if g < 2 else nc.scalar.copy)
             x_codes = held.tile([P, HALF], U32, name="x_codes%d_%d" % (g, h), align_bytes=64)
             x_planes = held.tile([P, HALF], U8, name="x_planes%d_%d" % (g, h), align_bytes=64)
             nc.vector.quantize_mx(

@@ -78,10 +78,14 @@ def tile_routed_moe_kernel(tc, xT, w_words, w_scales, b, gate, offs, out):
                 paired[(g, h)] = held.tile([P, 2, HALF, 2], BF16, name="pair%d_%d" % (g, h), align_bytes=64)
             return paired[(g, h)]
 
-        def merge(g, h, engine_copy):
-            grouped[(g, h)] = held.tile([P, HALF, PACK], BF16, name="grp%d_%d" % (g, h), align_bytes=64)
-            engine_copy(
-                out=grouped[(g, h)][:].rearrange("p s t -> p (s t)").bitcast(F32).rearrange("p (s u) -> p s u", u=2),
+        def group_tile(g, h):
+            if (g, h) not in grouped:
+                grouped[(g, h)] = held.tile([P, HALF, PACK], BF16, name="grp%d_%d" % (g, h), align_bytes=64)
+            return grouped[(g, h)]
+
+        def merge(g, h):
+            nc.vector.tensor_copy(
+                out=group_tile(g, h)[:].rearrange("p s t -> p (s t)").bitcast(F32).rearrange("p (s u) -> p s u", u=2),
                 in_=paired[(g, h)][:].rearrange("p u s e -> p (u s e)").bitcast(F32).rearrange("p (u s) -> p s u", u=2),
             )
 
@@ -92,10 +96,11 @@ def tile_routed_moe_kernel(tc, xT, w_words, w_scales, b, gate, offs, out):
             nc.vector.tensor_copy(out=pair_tile(g, h)[:, t // 2, :, t % 2], in_=raw[g][:, t, :].indirect(offs_of(h)))
 
         def gather_s(g, t, h):
-            nc.scalar.activation(out=pair_tile(g, h)[:, t // 2, :, t % 2], in_=xb[g][:, t, :].indirect(offs_of(h)), func=copy)
+            nc.scalar.activation(out=group_tile(g, h)[:, :, t], in_=xb[g][:, t, :].indirect(offs_of(h)), func=copy)
 
         def multiply(g, h):
-            merge(g, h, nc.vector.tensor_copy if g < 2 else nc.scalar.copy)
+            if g < 2:
+                merge(g, h)
             x_codes = held.tile([P, HALF], U32, name="x_codes%d_%d" % (g, h), align_bytes=64)
             x_planes = held.tile([P, HALF], U8, name="x_planes%d_%d" % (g, h), align_bytes=64)
             nc.vector.quantize_mx(

@@ -17,8 +17,6 @@ P = 128
 PACK = 4
 PASSES = K // (P * PACK)
 
-HALF = 256
-
 
 def tile_routed_moe_kernel(tc, xT, w_words, w_scales, b, gate, offs, out):
     nc = tc.nc
@@ -29,6 +27,7 @@ def tile_routed_moe_kernel(tc, xT, w_words, w_scales, b, gate, offs, out):
 
     with ExitStack() as ctx:
         held = ctx.enter_context(tc.tile_pool(name="held", bufs=1))
+        turn = ctx.enter_context(tc.tile_pool(name="turn", bufs=1))
         psum = ctx.enter_context(tc.psum_pool(name="psum", bufs=1))
 
         offsets = held.tile([P, E * C // 16], U16, name="offsets")
@@ -58,56 +57,60 @@ def tile_routed_moe_kernel(tc, xT, w_words, w_scales, b, gate, offs, out):
         for a in (0, 2, 1, 3):
             w_codes[a] = held.tile([P, E, N], U32, name="w_codes%d" % a, align_bytes=64)
             nc.sync.dma_start(w_codes[a][:].bitcast(I32), w_view[a])
-        b_sb = held.tile([P, E], F32, name="b_sb")
-        nc.sync.dma_start(b_sb[:], b)
+        b_first = turn.tile([P, 2], F32, name="turn", align_bytes=64)
+        nc.sync.dma_start(b_first[:], b[:, 0:2])
+        b_last = held.tile([P, 2], F32, name="b_last")
+        nc.sync.dma_start(b_last[:], b[:, 2:4])
         gate_sb = held.tile([P, E * C], F32, name="gate_sb")
         nc.sync.dma_start(gate_sb[:], gate)
 
         acc = [psum.tile([P, C], F32, name="acc%d" % e) for e in range(E)]
         window = held.tile([P, T], F32, name="window")
+        y = [held.tile([P, C], F32, name="y%d" % e) for e in range(E)]
+        y01 = held.tile([P, 2 * C], F32, name="y01")
         grouped = {}
+        paired = {}
         pass_order = (0, 2, 1, 3)
 
-        def offs_of(h):
-            return offsets[:, h * (HALF // 16) : (h + 1) * (HALF // 16)]
+        def offs_of(e0, ne):
+            return offsets[:, e0 * (C // 16) : (e0 + ne) * (C // 16)]
 
-        paired = {}
+        def group_tile(piece):
+            if piece not in grouped:
+                grouped[piece] = held.tile([P, piece[2] * C, PACK], BF16, name="grp%d_%d" % piece[:2], align_bytes=64)
+            return grouped[piece]
 
-        def pair_tile(g, h):
-            if (g, h) not in paired:
-                paired[(g, h)] = held.tile([P, 2, HALF, 2], BF16, name="pair%d_%d" % (g, h), align_bytes=64)
-            return paired[(g, h)]
-
-        def group_tile(g, h):
-            if (g, h) not in grouped:
-                grouped[(g, h)] = held.tile([P, HALF, PACK], BF16, name="grp%d_%d" % (g, h), align_bytes=64)
-            return grouped[(g, h)]
-
-        def merge(g, h):
-            nc.vector.tensor_copy(
-                out=group_tile(g, h)[:].rearrange("p s t -> p (s t)").bitcast(F32).rearrange("p (s u) -> p s u", u=2),
-                in_=paired[(g, h)][:].rearrange("p u s e -> p (u s e)").bitcast(F32).rearrange("p (u s) -> p s u", u=2),
-            )
+        def pair_tile(piece):
+            if piece not in paired:
+                paired[piece] = held.tile([P, 2, piece[2] * C, 2], BF16, name="pair%d_%d" % piece[:2], align_bytes=64)
+            return paired[piece]
 
         def cast(g, t):
             nc.gpsimd.tensor_scalar(out=xb[g][:, t, :], in0=raw[g][:, t, :], scalar1=1.0, scalar2=0.0, op0=mult, op1=add)
 
-        def gather_v(g, t, h):
-            nc.vector.tensor_copy(out=pair_tile(g, h)[:, t // 2, :, t % 2], in_=raw[g][:, t, :].indirect(offs_of(h)))
+        def gather_v(piece, t):
+            nc.vector.tensor_copy(out=pair_tile(piece)[:, t // 2, :, t % 2], in_=raw[piece[0]][:, t, :].indirect(offs_of(*piece[1:])))
 
-        def gather_s(g, t, h):
-            nc.scalar.activation(out=group_tile(g, h)[:, :, t], in_=xb[g][:, t, :].indirect(offs_of(h)), func=copy)
+        def gather_s(piece, t):
+            nc.scalar.activation(out=group_tile(piece)[:, :, t], in_=xb[piece[0]][:, t, :].indirect(offs_of(*piece[1:])), func=copy)
 
-        def multiply(g, h):
-            if g < 2:
-                merge(g, h)
-            x_codes = held.tile([P, HALF], U32, name="x_codes%d_%d" % (g, h), align_bytes=64)
-            x_planes = held.tile([P, HALF], U8, name="x_planes%d_%d" % (g, h), align_bytes=64)
-            nc.vector.quantize_mx(
-                out=x_codes[:].bitcast(FP8X4), scales=x_planes[:], in_=grouped[(g, h)][:].rearrange("p n t -> p (n t)")
+        def merge(piece):
+            nc.vector.tensor_copy(
+                out=group_tile(piece)[:].rearrange("p s t -> p (s t)").bitcast(F32).rearrange("p (s u) -> p s u", u=2),
+                in_=paired[piece][:].rearrange("p u s e -> p (u s e)").bitcast(F32).rearrange("p (u s) -> p s u", u=2),
             )
-            for i in range(HALF // C):
-                e = h * (HALF // C) + i
+
+        def multiply(piece):
+            g, e0, ne = piece
+            if piece in paired:
+                merge(piece)
+            x_codes = held.tile([P, ne * C], U32, name="x_codes%d_%d" % (g, e0), align_bytes=64)
+            x_planes = held.tile([P, ne * C], U8, name="x_planes%d_%d" % (g, e0), align_bytes=64)
+            nc.vector.quantize_mx(
+                out=x_codes[:].bitcast(FP8X4), scales=x_planes[:], in_=grouped[piece][:].rearrange("p n t -> p (n t)")
+            )
+            for i in range(ne):
+                e = e0 + i
                 nc.tensor.matmul_mx(
                     out=acc[e][:],
                     lhsT=w_codes[g][:, e, :].bitcast(FP8X4),
@@ -118,51 +121,44 @@ def tile_routed_moe_kernel(tc, xT, w_words, w_scales, b, gate, offs, out):
                     stop=(g == pass_order[-1]),
                 )
 
-        y = [held.tile([P, HALF], F32, name="y%d" % h) for h in range(2)]
-
-        def activate(h):
-            for i in range(HALF // C):
-                e = h * (HALF // C) + i
-                nc.scalar.activation(out=y[h][:, i * C : (i + 1) * C], in_=acc[e][:], func=silu, bias=b_sb[:, e : e + 1])
-
-        def scatter(h):
-            nc.vector.tensor_tensor(
-                out=window[:].indirect(offs_of(h)), in0=y[h][:], in1=gate_sb[:, h * HALF : (h + 1) * HALF], op=mult
-            )
-
         for g in (2, 3):
             for t in range(PACK):
                 cast(g, t)
         for t in range(PACK):
-            for h in range(2):
-                gather_v(0, t, h)
+            for e0 in (0, 2):
+                gather_v((0, e0, 2), t)
         for t in range(PACK):
-            for h in range(2):
-                gather_s(2, t, h)
-        gather_v(1, 0, 0)
-        multiply(0, 0)
-        gather_v(1, 0, 1)
-        multiply(0, 1)
+            for e0 in (0, 2):
+                gather_s((2, e0, 2), t)
+        gather_v((1, 0, 2), 0)
+        multiply((0, 0, 2))
+        gather_v((1, 2, 2), 0)
+        multiply((0, 2, 2))
         for t in (1, 2):
-            for h in range(2):
-                gather_v(1, t, h)
-        multiply(2, 0)
-        gather_v(1, 3, 0)
-        multiply(2, 1)
-        gather_v(1, 3, 1)
+            for e0 in (0, 2):
+                gather_v((1, e0, 2), t)
+        multiply((2, 0, 2))
+        gather_v((1, 0, 2), 3)
+        multiply((2, 2, 2))
+        gather_v((1, 2, 2), 3)
         for t in range(PACK):
-            gather_s(3, t, 0)
-        multiply(1, 0)
-        multiply(1, 1)
-        multiply(3, 0)
-        gather_s(3, 0, 1)
-        gather_s(3, 1, 1)
-        activate(0)
-        gather_s(3, 2, 1)
-        gather_s(3, 3, 1)
-        scatter(0)
-        multiply(3, 1)
-        activate(1)
-        scatter(1)
+            gather_s((3, 0, 2), t)
+        multiply((1, 0, 2))
+        multiply((3, 0, 2))
+        multiply((1, 2, 2))
+        for t in range(PACK):
+            gather_s((3, 2, 1), t)
+        for e in (0, 1):
+            nc.scalar.activation(out=y01[:, e * C : (e + 1) * C], in_=acc[e][:], func=silu, bias=b_first[:, e : e + 1])
+        nc.vector.tensor_tensor(out=window[:].indirect(offs_of(0, 2)), in0=y01[:], in1=gate_sb[:, 0 : 2 * C], op=mult)
+        grouped[(3, 3, 1)] = turn.tile([P, C, PACK], BF16, name="turn", align_bytes=64)
+        for t in range(PACK):
+            gather_s((3, 3, 1), t)
+        multiply((3, 2, 1))
+        nc.scalar.activation(out=y[2][:], in_=acc[2][:], func=silu, bias=b_last[:, 0:1])
+        multiply((3, 3, 1))
+        nc.vector.tensor_tensor(out=window[:].indirect(offs_of(2, 1)), in0=y[2][:], in1=gate_sb[:, 2 * C : 3 * C], op=mult)
+        nc.scalar.activation(out=y[3][:], in_=acc[3][:], func=silu, bias=b_last[:, 1:2])
+        nc.vector.tensor_tensor(out=window[:].indirect(offs_of(3, 1)), in0=y[3][:], in1=gate_sb[:, 3 * C : 4 * C], op=mult)
 
         nc.sync.dma_start(out, window[:])

@@ -16,6 +16,14 @@ FP8X4 = mybir.dt.float8_e4m3fn_x4
 P = 128
 PACK = 4
 PASSES = K // (P * PACK)
+PER_COLUMN = 16
+
+VECTOR_PASSES = (0, 1)
+SCALAR_PASSES = (2, 3)
+PASS_ORDER = (0, 2, 1, 3)
+FIRST_HALF = (0, 2)
+SECOND_HALF = (2, 2)
+LAST_PIECES = ((3, 2, 1), (3, 3, 1))
 
 
 def tile_routed_moe_kernel(tc, xT, w_words, w_scales, b, gate, offs, out):
@@ -27,10 +35,10 @@ def tile_routed_moe_kernel(tc, xT, w_words, w_scales, b, gate, offs, out):
 
     with ExitStack() as ctx:
         held = ctx.enter_context(tc.tile_pool(name="held", bufs=1))
-        turn = ctx.enter_context(tc.tile_pool(name="turn", bufs=1))
+        handed = ctx.enter_context(tc.tile_pool(name="handed", bufs=1))
         psum = ctx.enter_context(tc.psum_pool(name="psum", bufs=1))
 
-        offsets = held.tile([P, E * C // 16], U16, name="offsets")
+        offsets = held.tile([P, E * C // PER_COLUMN], U16, name="offsets")
         nc.sync.dma_start(offsets[:], offs)
 
         zero = held.tile([P, 1], F32, name="zero")
@@ -38,127 +46,128 @@ def tile_routed_moe_kernel(tc, xT, w_words, w_scales, b, gate, offs, out):
         nc.gpsimd.memset(zero[:], 0.0)
         nc.scalar.activation(out=warm[:], in_=zero[:], func=silu)
 
-        w_planes = held.tile([P, E * PASSES, N], U8, name="w_planes", align_bytes=64)
-        nc.vector.memset(w_planes[:].rearrange("p a n -> p (a n)").bitcast(I32), 0)
+        w_scale_sb = held.tile([P, E * PASSES, N], U8, name="w_scale_sb", align_bytes=64)
+        nc.vector.memset(w_scale_sb[:].rearrange("p a n -> p (a n)").bitcast(I32), 0)
 
         x_view = xT.rearrange("(g p t) n -> g p t n", p=P, t=PACK)
-        raw = [held.tile([P, PACK, T], F32, name="raw%d" % g) for g in range(PASSES)]
-        xb = {g: held.tile([P, PACK, T], BF16, name="xb%d" % g) for g in (2, 3)}
-
-        for i in range(8):
-            for g in (i // PACK, 2 + i // PACK):
-                nc.sync.dma_start(raw[g][:, i % PACK, :], x_view[g, :, i % PACK, :])
+        x_f32 = [held.tile([P, PACK, T], F32, name="x_f32_%d" % g) for g in range(PASSES)]
+        x_bf16 = {g: held.tile([P, PACK, T], BF16, name="x_bf16_%d" % g) for g in SCALAR_PASSES}
+        for g_vector, g_scalar in zip(VECTOR_PASSES, SCALAR_PASSES):
+            for t in range(PACK):
+                for g in (g_vector, g_scalar):
+                    nc.sync.dma_start(x_f32[g][:, t, :], x_view[g, :, t, :])
 
         s_view = w_scales.bitcast(I32).rearrange("e a (q r) n -> r q (e a) n", r=4)
         for r in range(4):
-            nc.sync.dma_start(w_planes[r:P:32, :, :].bitcast(I32), s_view[r])
+            nc.sync.dma_start(w_scale_sb[r:P:32, :, :].bitcast(I32), s_view[r])
         w_view = w_words.rearrange("e a p n r -> a p e (n r)").bitcast(I32)
         w_codes = {}
-        for a in (0, 2, 1, 3):
+        for a in PASS_ORDER:
             w_codes[a] = held.tile([P, E, N], U32, name="w_codes%d" % a, align_bytes=64)
             nc.sync.dma_start(w_codes[a][:].bitcast(I32), w_view[a])
-        b_first = turn.tile([P, 2], F32, name="turn", align_bytes=64)
-        nc.sync.dma_start(b_first[:], b[:, 0:2])
-        b_last = held.tile([P, 2], F32, name="b_last")
-        nc.sync.dma_start(b_last[:], b[:, 2:4])
+        bias = {
+            FIRST_HALF: handed.tile([P, 2], F32, name="handed_on", align_bytes=64),
+            SECOND_HALF: held.tile([P, 2], F32, name="bias_second"),
+        }
+        for e0, ne in (FIRST_HALF, SECOND_HALF):
+            nc.sync.dma_start(bias[(e0, ne)][:], b[:, e0 : e0 + ne])
         gate_sb = held.tile([P, E * C], F32, name="gate_sb")
         nc.sync.dma_start(gate_sb[:], gate)
 
         acc = [psum.tile([P, C], F32, name="acc%d" % e) for e in range(E)]
         window = held.tile([P, T], F32, name="window")
-        y = [held.tile([P, C], F32, name="y%d" % e) for e in range(E)]
-        y01 = held.tile([P, 2 * C], F32, name="y01")
         grouped = {}
         paired = {}
-        pass_order = (0, 2, 1, 3)
 
-        def offs_of(e0, ne):
-            return offsets[:, e0 * (C // 16) : (e0 + ne) * (C // 16)]
+        def offsets_of(e0, ne):
+            return offsets[:, e0 * C // PER_COLUMN : (e0 + ne) * C // PER_COLUMN]
 
-        def group_tile(piece):
+        def grouped_tile(piece):
             if piece not in grouped:
-                grouped[piece] = held.tile([P, piece[2] * C, PACK], BF16, name="grp%d_%d" % piece[:2], align_bytes=64)
+                grouped[piece] = held.tile([P, piece[2] * C, PACK], BF16, name="grouped%d_%d" % piece[:2], align_bytes=64)
             return grouped[piece]
 
-        def pair_tile(piece):
+        def round_plane(g, t):
+            nc.gpsimd.tensor_scalar(out=x_bf16[g][:, t, :], in0=x_f32[g][:, t, :], scalar1=1.0, scalar2=0.0, op0=mult, op1=add)
+
+        def gather_on_vector(piece, t):
+            g, e0, ne = piece
             if piece not in paired:
-                paired[piece] = held.tile([P, 2, piece[2] * C, 2], BF16, name="pair%d_%d" % piece[:2], align_bytes=64)
-            return paired[piece]
+                paired[piece] = held.tile([P, 2, ne * C, 2], BF16, name="paired%d_%d" % (g, e0), align_bytes=64)
+            nc.vector.tensor_copy(out=paired[piece][:, t // 2, :, t % 2], in_=x_f32[g][:, t, :].indirect(offsets_of(e0, ne)))
 
-        def cast(g, t):
-            nc.gpsimd.tensor_scalar(out=xb[g][:, t, :], in0=raw[g][:, t, :], scalar1=1.0, scalar2=0.0, op0=mult, op1=add)
+        def gather_on_scalar(piece, t):
+            g, e0, ne = piece
+            nc.scalar.activation(out=grouped_tile(piece)[:, :, t], in_=x_bf16[g][:, t, :].indirect(offsets_of(e0, ne)), func=copy)
 
-        def gather_v(piece, t):
-            nc.vector.tensor_copy(out=pair_tile(piece)[:, t // 2, :, t % 2], in_=raw[piece[0]][:, t, :].indirect(offs_of(*piece[1:])))
-
-        def gather_s(piece, t):
-            nc.scalar.activation(out=group_tile(piece)[:, :, t], in_=xb[piece[0]][:, t, :].indirect(offs_of(*piece[1:])), func=copy)
-
-        def merge(piece):
+        def interleave_pairs(piece):
             nc.vector.tensor_copy(
-                out=group_tile(piece)[:].rearrange("p s t -> p (s t)").bitcast(F32).rearrange("p (s u) -> p s u", u=2),
-                in_=paired[piece][:].rearrange("p u s e -> p (u s e)").bitcast(F32).rearrange("p (u s) -> p s u", u=2),
+                out=grouped_tile(piece)[:].rearrange("p s t -> p (s t)").bitcast(F32).rearrange("p (s u) -> p s u", u=2),
+                in_=paired[piece][:].rearrange("p u s i -> p (u s i)").bitcast(F32).rearrange("p (u s) -> p s u", u=2),
             )
 
         def multiply(piece):
             g, e0, ne = piece
             if piece in paired:
-                merge(piece)
+                interleave_pairs(piece)
             x_codes = held.tile([P, ne * C], U32, name="x_codes%d_%d" % (g, e0), align_bytes=64)
-            x_planes = held.tile([P, ne * C], U8, name="x_planes%d_%d" % (g, e0), align_bytes=64)
+            x_scale_sb = held.tile([P, ne * C], U8, name="x_scale_sb%d_%d" % (g, e0), align_bytes=64)
             nc.vector.quantize_mx(
-                out=x_codes[:].bitcast(FP8X4), scales=x_planes[:], in_=grouped[piece][:].rearrange("p n t -> p (n t)")
+                out=x_codes[:].bitcast(FP8X4), scales=x_scale_sb[:], in_=grouped[piece][:].rearrange("p s t -> p (s t)")
             )
             for i in range(ne):
                 e = e0 + i
                 nc.tensor.matmul_mx(
                     out=acc[e][:],
                     lhsT=w_codes[g][:, e, :].bitcast(FP8X4),
-                    lhsT_scale=w_planes[:, e * PASSES + g, :],
+                    lhsT_scale=w_scale_sb[:, e * PASSES + g, :],
                     rhs=x_codes[:, i * C : (i + 1) * C].bitcast(FP8X4),
-                    rhs_scale=x_planes[:, i * C : (i + 1) * C],
-                    start=(g == pass_order[0]),
-                    stop=(g == pass_order[-1]),
+                    rhs_scale=x_scale_sb[:, i * C : (i + 1) * C],
+                    start=(g == PASS_ORDER[0]),
+                    stop=(g == PASS_ORDER[-1]),
                 )
 
-        for g in (2, 3):
+        def finish(e0, ne, half):
+            activated = held.tile([P, ne * C], F32, name="activated%d" % e0)
+            for i in range(ne):
+                e = e0 + i
+                nc.scalar.activation(
+                    out=activated[:, i * C : (i + 1) * C], in_=acc[e][:], func=silu, bias=bias[half][:, e - half[0] : e - half[0] + 1]
+                )
+            nc.vector.tensor_tensor(
+                out=window[:].indirect(offsets_of(e0, ne)), in0=activated[:], in1=gate_sb[:, e0 * C : (e0 + ne) * C], op=mult
+            )
+
+        for g in SCALAR_PASSES:
             for t in range(PACK):
-                cast(g, t)
+                round_plane(g, t)
         for t in range(PACK):
-            for e0 in (0, 2):
-                gather_v((0, e0, 2), t)
+            for half in (FIRST_HALF, SECOND_HALF):
+                gather_on_vector((0,) + half, t)
         for t in range(PACK):
-            for e0 in (0, 2):
-                gather_s((2, e0, 2), t)
-        gather_v((1, 0, 2), 0)
-        multiply((0, 0, 2))
-        gather_v((1, 2, 2), 0)
-        multiply((0, 2, 2))
-        for t in (1, 2):
-            for e0 in (0, 2):
-                gather_v((1, e0, 2), t)
-        multiply((2, 0, 2))
-        gather_v((1, 0, 2), 3)
-        multiply((2, 2, 2))
-        gather_v((1, 2, 2), 3)
+            for half in (FIRST_HALF, SECOND_HALF):
+                gather_on_scalar((2,) + half, t)
+
         for t in range(PACK):
-            gather_s((3, 0, 2), t)
-        multiply((1, 0, 2))
-        multiply((3, 0, 2))
-        multiply((1, 2, 2))
+            gather_on_vector((1,) + FIRST_HALF, t)
         for t in range(PACK):
-            gather_s((3, 2, 1), t)
-        for e in (0, 1):
-            nc.scalar.activation(out=y01[:, e * C : (e + 1) * C], in_=acc[e][:], func=silu, bias=b_first[:, e : e + 1])
-        nc.vector.tensor_tensor(out=window[:].indirect(offs_of(0, 2)), in0=y01[:], in1=gate_sb[:, 0 : 2 * C], op=mult)
-        grouped[(3, 3, 1)] = turn.tile([P, C, PACK], BF16, name="turn", align_bytes=64)
+            gather_on_scalar((3,) + FIRST_HALF, t)
+        for g in PASS_ORDER:
+            multiply((g,) + FIRST_HALF)
         for t in range(PACK):
-            gather_s((3, 3, 1), t)
-        multiply((3, 2, 1))
-        nc.scalar.activation(out=y[2][:], in_=acc[2][:], func=silu, bias=b_last[:, 0:1])
-        multiply((3, 3, 1))
-        nc.vector.tensor_tensor(out=window[:].indirect(offs_of(2, 1)), in0=y[2][:], in1=gate_sb[:, 2 * C : 3 * C], op=mult)
-        nc.scalar.activation(out=y[3][:], in_=acc[3][:], func=silu, bias=b_last[:, 1:2])
-        nc.vector.tensor_tensor(out=window[:].indirect(offs_of(3, 1)), in0=y[3][:], in1=gate_sb[:, 3 * C : 4 * C], op=mult)
+            gather_on_vector((1,) + SECOND_HALF, t)
+        for t in range(PACK):
+            gather_on_scalar(LAST_PIECES[0], t)
+        finish(*FIRST_HALF, FIRST_HALF)
+
+        grouped[LAST_PIECES[1]] = handed.tile([P, C, PACK], BF16, name="handed_on", align_bytes=64)
+        for t in range(PACK):
+            gather_on_scalar(LAST_PIECES[1], t)
+        for g in PASS_ORDER[:-1]:
+            multiply((g,) + SECOND_HALF)
+        for piece in LAST_PIECES:
+            multiply(piece)
+        for piece in LAST_PIECES:
+            finish(piece[1], piece[2], SECOND_HALF)
 
         nc.sync.dma_start(out, window[:])

@@ -39,7 +39,6 @@ def tile_routed_moe_kernel(tc, xT, w_words, w_scales, b, gate, offs, out):
         psum = ctx.enter_context(tc.psum_pool(name="psum", bufs=1))
 
         offsets = held.tile([P, E * C // PER_COLUMN], U16, name="offsets")
-        nc.sync.dma_start(offsets[:], offs)
 
         zero = held.tile([P, 1], F32, name="zero")
         warm = held.tile([P, 1], F32, name="warm")
@@ -56,6 +55,8 @@ def tile_routed_moe_kernel(tc, xT, w_words, w_scales, b, gate, offs, out):
             for t in range(PACK):
                 for g in (g_vector, g_scalar):
                     nc.sync.dma_start(x_f32[g][:, t, :], x_view[g, :, t, :])
+                    if (g, t) == (VECTOR_PASSES[0], 0):
+                        nc.sync.dma_start(offsets[:], offs)
 
         s_view = w_scales.bitcast(I32).rearrange("e a (q r) n -> r q (e a) n", r=4)
         for r in range(4):

from contextlib import ExitStack

import concourse.mybir as mybir

K, T, E, C, N = 2048, 512, 4, 128, 128
FLOPS = 2 * K * N * E * C

F32 = mybir.dt.float32
BF16 = mybir.dt.bfloat16
I32 = mybir.dt.int32
U32 = mybir.dt.uint32
U16 = mybir.dt.uint16
U8 = mybir.dt.uint8
FP8X4 = mybir.dt.float8_e4m3fn_x4

P = 128
PACK = 4
PASSES = K // (P * PACK)
PER_COLUMN = 16

VECTOR_PASSES = (0, 1)
SCALAR_PASSES = (2, 3)
PASS_ORDER = (0, 2, 1, 3)
FIRST_HALF = (0, 2)
SECOND_HALF = (2, 2)
LAST_PIECES = ((3, 2, 1), (3, 3, 1))


def tile_routed_moe_kernel(tc, xT, w_words, w_scales, b, gate, offs, out):
    nc = tc.nc
    silu = mybir.ActivationFunctionType.Silu
    copy = mybir.ActivationFunctionType.Copy
    mult = mybir.AluOpType.mult
    add = mybir.AluOpType.add

    with ExitStack() as ctx:
        held = ctx.enter_context(tc.tile_pool(name="held", bufs=1))
        handed = ctx.enter_context(tc.tile_pool(name="handed", bufs=1))
        psum = ctx.enter_context(tc.psum_pool(name="psum", bufs=1))

        offsets = held.tile([P, E * C // PER_COLUMN], U16, name="offsets")

        zero = held.tile([P, 1], F32, name="zero")
        warm = held.tile([P, 1], F32, name="warm")
        nc.gpsimd.memset(zero[:], 0.0)
        nc.scalar.activation(out=warm[:], in_=zero[:], func=silu)

        w_scale_sb = held.tile([P, E * PASSES, N], U8, name="w_scale_sb", align_bytes=64)
        nc.vector.memset(w_scale_sb[:].rearrange("p a n -> p (a n)").bitcast(I32), 0)

        x_view = xT.rearrange("(g p t) n -> g p t n", p=P, t=PACK)
        x_f32 = [held.tile([P, PACK, T], F32, name="x_f32_%d" % g) for g in range(PASSES)]
        x_bf16 = {g: held.tile([P, PACK, T], BF16, name="x_bf16_%d" % g) for g in SCALAR_PASSES}
        for g_vector, g_scalar in zip(VECTOR_PASSES, SCALAR_PASSES):
            for t in range(PACK):
                for g in (g_vector, g_scalar):
                    nc.sync.dma_start(x_f32[g][:, t, :], x_view[g, :, t, :])
                    if (g, t) == (VECTOR_PASSES[0], 0):
                        nc.sync.dma_start(offsets[:], offs)

        s_view = w_scales.bitcast(I32).rearrange("e a (q r) n -> r q (e a) n", r=4)
        for r in range(4):
            nc.sync.dma_start(w_scale_sb[r:P:32, :, :].bitcast(I32), s_view[r])
        w_view = w_words.rearrange("e a p n r -> a p e (n r)").bitcast(I32)
        w_codes = {}
        for a in PASS_ORDER:
            w_codes[a] = held.tile([P, E, N], U32, name="w_codes%d" % a, align_bytes=64)
            nc.sync.dma_start(w_codes[a][:].bitcast(I32), w_view[a])
        bias = {
            FIRST_HALF: handed.tile([P, 2], F32, name="handed_on", align_bytes=64),
            SECOND_HALF: held.tile([P, 2], F32, name="bias_second"),
        }
        for e0, ne in (FIRST_HALF, SECOND_HALF):
            nc.sync.dma_start(bias[(e0, ne)][:], b[:, e0 : e0 + ne])
        gate_sb = held.tile([P, E * C], F32, name="gate_sb")
        nc.sync.dma_start(gate_sb[:], gate)

        acc = [psum.tile([P, C], F32, name="acc%d" % e) for e in range(E)]
        window = held.tile([P, T], F32, name="window")
        grouped = {}
        paired = {}

        def offsets_of(e0, ne):
            return offsets[:, e0 * C // PER_COLUMN : (e0 + ne) * C // PER_COLUMN]

        def grouped_tile(piece):
            if piece not in grouped:
                grouped[piece] = held.tile([P, piece[2] * C, PACK], BF16, name="grouped%d_%d" % piece[:2], align_bytes=64)
            return grouped[piece]

        def round_plane(g, t):
            nc.gpsimd.tensor_scalar(out=x_bf16[g][:, t, :], in0=x_f32[g][:, t, :], scalar1=1.0, scalar2=0.0, op0=mult, op1=add)

        def gather_on_vector(piece, t):
            g, e0, ne = piece
            if piece not in paired:
                paired[piece] = held.tile([P, 2, ne * C, 2], BF16, name="paired%d_%d" % (g, e0), align_bytes=64)
            nc.vector.tensor_copy(out=paired[piece][:, t // 2, :, t % 2], in_=x_f32[g][:, t, :].indirect(offsets_of(e0, ne)))

        def gather_on_scalar(piece, t):
            g, e0, ne = piece
            nc.scalar.activation(out=grouped_tile(piece)[:, :, t], in_=x_bf16[g][:, t, :].indirect(offsets_of(e0, ne)), func=copy)

        def interleave_pairs(piece):
            nc.vector.tensor_copy(
                out=grouped_tile(piece)[:].rearrange("p s t -> p (s t)").bitcast(F32).rearrange("p (s u) -> p s u", u=2),
                in_=paired[piece][:].rearrange("p u s i -> p (u s i)").bitcast(F32).rearrange("p (u s) -> p s u", u=2),
            )

        def multiply(piece):
            g, e0, ne = piece
            if piece in paired:
                interleave_pairs(piece)
            x_codes = held.tile([P, ne * C], U32, name="x_codes%d_%d" % (g, e0), align_bytes=64)
            x_scale_sb = held.tile([P, ne * C], U8, name="x_scale_sb%d_%d" % (g, e0), align_bytes=64)
            nc.vector.quantize_mx(
                out=x_codes[:].bitcast(FP8X4), scales=x_scale_sb[:], in_=grouped[piece][:].rearrange("p s t -> p (s t)")
            )
            for i in range(ne):
                e = e0 + i
                nc.tensor.matmul_mx(
                    out=acc[e][:],
                    lhsT=w_codes[g][:, e, :].bitcast(FP8X4),
                    lhsT_scale=w_scale_sb[:, e * PASSES + g, :],
                    rhs=x_codes[:, i * C : (i + 1) * C].bitcast(FP8X4),
                    rhs_scale=x_scale_sb[:, i * C : (i + 1) * C],
                    start=(g == PASS_ORDER[0]),
                    stop=(g == PASS_ORDER[-1]),
                )

        def finish(e0, ne, half):
            activated = held.tile([P, ne * C], F32, name="activated%d" % e0)
            for i in range(ne):
                e = e0 + i
                nc.scalar.activation(
                    out=activated[:, i * C : (i + 1) * C], in_=acc[e][:], func=silu, bias=bias[half][:, e - half[0] : e - half[0] + 1]
                )
            nc.vector.tensor_tensor(
                out=window[:].indirect(offsets_of(e0, ne)), in0=activated[:], in1=gate_sb[:, e0 * C : (e0 + ne) * C], op=mult
            )

        for g in SCALAR_PASSES:
            for t in range(PACK):
                round_plane(g, t)
        for t in range(PACK):
            for half in (FIRST_HALF, SECOND_HALF):
                gather_on_vector((0,) + half, t)
        for t in range(PACK):
            for half in (FIRST_HALF, SECOND_HALF):
                gather_on_scalar((2,) + half, t)

        for t in range(PACK):
            gather_on_vector((1,) + FIRST_HALF, t)
        for t in range(PACK):
            gather_on_scalar((3,) + FIRST_HALF, t)
        for g in PASS_ORDER:
            multiply((g,) + FIRST_HALF)
        for t in range(PACK):
            gather_on_vector((1,) + SECOND_HALF, t)
        for t in range(PACK):
            gather_on_scalar(LAST_PIECES[0], t)
        finish(*FIRST_HALF, FIRST_HALF)

        grouped[LAST_PIECES[1]] = handed.tile([P, C, PACK], BF16, name="handed_on", align_bytes=64)
        for t in range(PACK):
            gather_on_scalar(LAST_PIECES[1], t)
        for g in PASS_ORDER[:-1]:
            multiply((g,) + SECOND_HALF)
        for piece in LAST_PIECES:
            multiply(piece)
        for piece in LAST_PIECES:
            finish(piece[1], piece[2], SECOND_HALF)

        nc.sync.dma_start(out, window[:])
